import numpy as np
import ml_dtypes


def mxq(x, axis, fmt="e4m3"):
    dtype, down = {"e4m3": (ml_dtypes.float8_e4m3fn, 7), "e5m2": (ml_dtypes.float8_e5m2, 14)}[fmt]
    v = np.moveaxis(np.asarray(x, np.float32).astype(ml_dtypes.bfloat16).astype(np.float64), axis, -1)
    blocks = v.reshape(v.shape[:-1] + (-1, 32))
    amax = np.abs(blocks).max(-1, keepdims=True)
    byte = np.maximum(np.where(amax > 0, np.frexp(amax)[1] - 1 + 127, 0) - down, 1)
    scale = np.exp2(byte - 127.0)
    codes = (blocks / scale).astype(np.float32).astype(dtype).astype(np.float64)
    return np.moveaxis((codes * scale).reshape(v.shape), -1, axis)


WIDE = False


def mx_kscale(k):
    if not WIDE:
        return np.ones(k)
    levels = np.array([10, -10, 5, -5, 0])
    if k % 512:
        return np.exp2(np.random.permutation(np.resize(levels, k // 32))).repeat(32)
    a = np.empty((k // 512, 16))
    for p in range(k // 512):
        a[p, :8] = np.random.permutation(np.resize(levels, 8))
        for g in range(8):
            far = levels[np.abs(levels - a[p, g]) >= 10]
            a[p, g + 8] = far[np.random.randint(len(far))]
    return np.exp2(a.ravel()).repeat(32)


def f64(x):
    return np.asarray(x).astype(np.float64)


def striped(idx):
    return np.tile(idx.reshape(-1, 16).T, (8, 1)).astype(np.uint16)


def unstriped(offs):
    return offs[:16].T.reshape(-1).astype(np.int64)


def striped8(idx):
    return np.concatenate([x.reshape(-1, 16).T for x in idx]).astype(np.uint16)


def runs(offs, k):
    lists = np.stack([offs[16 * r : 16 * r + 16].T.reshape(-1) for r in range(8)]).astype(np.int64)
    return lists[np.arange(k) % 512 // 64]


def pack_weight(w):
    k, n = w.shape
    w = f64(np.asarray(w, np.float32).astype(ml_dtypes.bfloat16)).reshape(k // 32, 32, n)
    amax = np.abs(w).max(1)
    byte = np.clip(np.where(amax > 0, np.frexp(amax)[1] - 1 + 127 - 7, 1), 1, 254)
    scaled = (w * np.exp2(127.0 - byte)[:, None, :]).reshape(k, n).astype(np.float32)
    words = np.ascontiguousarray(scaled.reshape(k // 512, 128, 4, n).transpose(0, 1, 3, 2)).astype(ml_dtypes.float8_e4m3fn).view(np.uint8)
    return words, np.ascontiguousarray(byte.astype(np.uint8).reshape(k // 512, 16, n))


def unpack_weight(words, scales):
    g, p, n, _ = words.shape
    vals = np.ascontiguousarray(words).view(ml_dtypes.float8_e4m3fn).astype(np.float64) * np.repeat(np.exp2(scales.astype(np.float64) - 127.0), 8, axis=1)[..., None]
    return vals.transpose(0, 1, 3, 2).reshape(g * 512, n)


K, T, S, G, H, W, C, U = 512, 1024, 512, 2048, 512, 256, 512, 1024


def setup_inputs():
    n = np.random.standard_normal
    s = mx_kscale(K)[:, None]
    packed_xT = pack_weight(n((K, T)) * s)
    packed_dT = pack_weight(n((K, G)) / s)
    perm = np.stack([np.random.permutation(S) for _ in range(8)])
    perm2 = np.stack([np.random.permutation(U) for _ in range(8)])
    return {
        "x_words": packed_xT[0],
        "x_scales": packed_xT[1],
        "d_words": packed_dT[0],
        "d_scales": packed_dT[1],
        "gs": (np.random.uniform(0.5, 1.5, (K, 1)) / s).astype(np.float32),
        "offs": striped8(np.random.randint(0, T, (8, S))),
        "k1": striped8(np.random.randint(0, G, (8, H))),
        "n1": striped8(perm[:, :W]),
        "n2": striped8(perm[:, W:]),
        "cand": striped(np.random.permutation(T)[:C]),
        "n3": striped8(perm2[:, :S]),
        "n4": striped8(perm2[:, S:]),
        "n5": striped8(np.stack([np.random.permutation(S) for _ in range(8)])),
    }


def reference(x_words, x_scales, d_words, d_scales, gs, offs, k1, n1, n2, cand, n3, n4, n5):
    x_cand = unpack_weight(x_words, x_scales)[:, unstriped(cand)]
    d_k1 = unpack_weight(d_words, d_scales)[np.arange(K)[:, None], runs(k1, K)]
    xq = unpack_weight(x_words, x_scales)[np.arange(K)[:, None], runs(offs, K)]
    h = 0.0625 * (d_k1.T @ xq)
    pa = h[np.arange(H)[:, None], runs(n1, H)]
    pb = h[np.arange(H)[:, None], runs(n2, H)]
    ra = np.maximum(pa, pb)
    ds = h.copy()
    ds[np.arange(H)[:, None], runs(n1, H)] = ra
    z = f64(gs) * ds
    s = 0.0625 * ((x_cand.T @ mxq(z, 0, "e4m3")))
    dn = np.minimum(s, s[np.arange(C)[:, None], runs(n5, C)])
    up = np.maximum(s, s[np.arange(C)[:, None], runs(n5, C)])
    ph = np.zeros((C, U))
    ph[np.arange(C)[:, None], runs(n3, C)] = up
    out = ph.copy()
    out[np.arange(C)[:, None], runs(n4, C)] = dn
    return out

@@ -1,0 +1,183 @@
+from contextlib import ExitStack
+
+import concourse.mybir as mybir
+
+K, T, S, G, H, W, C, U = 512, 1024, 512, 2048, 512, 256, 512, 1024
+FLOPS = 2 * K * H * S + 2 * K * C * S
+
+F32 = mybir.dt.float32
+BF16 = mybir.dt.bfloat16
+I32 = mybir.dt.int32
+U32 = mybir.dt.uint32
+U16 = mybir.dt.uint16
+U8 = mybir.dt.uint8
+FP8X4 = mybir.dt.float8_e4m3fn_x4
+ACT = mybir.ActivationFunctionType
+ALU = mybir.AluOpType
+
+P = 128
+PACK = 4
+HALF = S // 2
+SIXTEENTH = 0.0625
+
+
+def tile_picked_hpqcfillpagmx_none_p_kernel(tc, x_words, x_scales, d_words, d_scales, gs, offs, k1, n1, n2, cand, n3, n4, n5, out):
+    nc = tc.nc
+    with ExitStack() as ctx:
+        keep = ctx.enter_context(tc.tile_pool(name="keep", bufs=1))
+        psum = ctx.enter_context(tc.psum_pool(name="psum", bufs=1))
+
+        def load_list(name, src):
+            tile = keep.tile([P, src.shape[1]], U16, name=name)
+            nc.sync.dma_start(tile[:], src)
+            return tile
+
+        def zeroed_bytes(name, width, engine):
+            tile = keep.tile([P, width], U8, name=name, align_bytes=64)
+            engine.memset(tile[:].bitcast(I32), 0)
+            return tile
+
+        def load_words(name, src, width):
+            tile = keep.tile([P, width], U32, name=name, align_bytes=64)
+            nc.sync.dma_start(tile[:].bitcast(I32), src[0].rearrange("p n t -> p (n t)").bitcast(I32))
+            return tile
+
+        d_sc = zeroed_bytes("d_sc", G, nc.gpsimd)
+        x_sc = zeroed_bytes("x_sc", T, nc.vector)
+        k1_t = load_list("k1_t", k1)
+        nc.sync.dma_start(d_sc[0:P:8, :].bitcast(I32), d_scales[0].bitcast(I32))
+        offs_t = load_list("offs_t", offs)
+        nc.sync.dma_start(x_sc[0:P:8, :].bitcast(I32), x_scales[0].bitcast(I32))
+        x_w = load_words("x_w", x_words, T)
+        d_w = load_words("d_w", d_words, G)
+        n1_t = load_list("n1_t", n1)
+        n2_t = load_list("n2_t", n2)
+        cand_t = load_list("cand_t", cand)
+        gs_t = keep.tile([P, PACK], F32, name="gs_t")
+        nc.gpsimd.dma_start(gs_t[:], gs.rearrange("(p t) o -> p (t o)", t=PACK))
+        n5_t = load_list("n5_t", n5)
+        n3_t = load_list("n3_t", n3)
+        n4_t = load_list("n4_t", n4)
+
+        def place_rows(name, src, queues):
+            plane = zeroed_bytes(name, src.shape[1], nc.vector)
+            for r in range(4):
+                queues[r % len(queues)].dma_start(plane[r:P:32, :].bitcast(I32), src[8 * r : P : 32, :].bitcast(I32))
+            return plane
+
+        picked_sc = keep.tile([P, H + S], U8, name="picked_sc", tag="picked_bytes", align_bytes=64)
+        nc.vector.tensor_copy(picked_sc[:, :H], d_sc[:].indirect(k1_t[:]))
+        nc.vector.tensor_copy(picked_sc[:, H:], x_sc[:].indirect(offs_t[:]))
+        placed_sc = place_rows("placed_sc", picked_sc, (nc.sync, nc.scalar))
+        xq_w = keep.tile([P, S], U32, name="xq_w", align_bytes=64)
+        nc.vector.tensor_copy(xq_w[:], x_w[:].indirect(offs_t[:]))
+        dk_w = keep.tile([P, H], U32, name="dk_w", align_bytes=64)
+        nc.vector.tensor_copy(dk_w[:], d_w[:].indirect(k1_t[:]))
+        dk_w_dealt = keep.tile([P, H], U32, name="dk_w_dealt", align_bytes=64)
+        nc.vector.tensor_copy(dk_w_dealt[:].rearrange("p (t m) -> p t m", t=PACK).bitcast(I32), dk_w[:].bitcast(I32).rearrange("p (m t) -> p t m", t=PACK))
+        dk_plane = keep.tile([P, H], U8, name="dk_plane", align_bytes=64)
+        nc.vector.tensor_copy(dk_plane[:].rearrange("p (t m) -> p t m", t=PACK), placed_sc[:, :H].rearrange("p (m t) -> p t m", t=PACK))
+
+        pages = []
+        for t in range(PACK):
+            page = keep.tile([P, U], F32, name=f"page{t}")
+            nc.gpsimd.memset(page[:], 0.0)
+            pages.append(page)
+
+        h_acc = []
+        for t in range(PACK):
+            cols = slice(t * P, (t + 1) * P)
+            acc = psum.tile([P, S], F32, name=f"h_acc{t}")
+            nc.tensor.matmul_mx(acc[:], lhsT=dk_w_dealt[:, cols].bitcast(FP8X4), lhsT_scale=dk_plane[:, cols],
+                                rhs=xq_w[:].bitcast(FP8X4), rhs_scale=placed_sc[:, H:], start=True, stop=True)
+            h_acc.append(acc)
+
+        xc_sc = keep.tile([P, C], U8, name="xc_sc", tag="picked_bytes", align_bytes=64)
+        nc.vector.tensor_copy(xc_sc[:].rearrange("p (t m) -> p m t", t=PACK), x_sc[:].indirect(cand_t[:]))
+        xc_plane = place_rows("xc_plane", xc_sc, (nc.sync,))
+
+        hs = []
+        for t in range(PACK):
+            h = keep.tile([P, S], F32, name=f"h{t}")
+            if t in (1, 2):
+                nc.vector.tensor_scalar_mul(h[:], h_acc[t][:], SIXTEENTH)
+            else:
+                nc.scalar.activation(h[:], h_acc[t][:], ACT.Copy, scale=SIXTEENTH)
+            hs.append(h)
+            pa = keep.tile([P, W], F32, name=f"pa{t}")
+            pb = keep.tile([P, W], F32, name=f"pb{t}")
+            nc.scalar.activation(pa[:], h[:].indirect(n1_t[:]), ACT.Copy)
+            nc.scalar.activation(pb[:], h[:].indirect(n2_t[:]), ACT.Copy)
+            ra = keep.tile([P, W], F32, name=f"ra{t}", align_bytes=64)
+            nc.vector.tensor_tensor(ra[:], pa[:], pb[:], ALU.max)
+            nc.vector.tensor_copy(h[:].indirect(n1_t[:]), ra[:])
+
+        xc_w = keep.tile([P, C], U32, name="xc_w", tag=f"ra{PACK - 1}", align_bytes=64)
+        nc.vector.tensor_copy(xc_w[:].rearrange("p (t m) -> p m t", t=PACK), x_w[:].indirect(cand_t[:]))
+
+        z_planes = [keep.tile([P, PACK, HALF], BF16, name=f"z_planes{b}", align_bytes=64) for b in range(2)]
+        for t in range(PACK):
+            for b in range(2):
+                nc.scalar.activation(z_planes[b][:, t, :], hs[t][:, b * HALF : (b + 1) * HALF], ACT.Copy, scale=gs_t[:, t : t + 1])
+
+        woven = []
+        for b in range(2):
+            wv = keep.tile([P, HALF, PACK], BF16, name=f"woven{b}", align_bytes=64)
+            nc.vector.tensor_copy(wv[:].rearrange("p (c i) t -> p c t i", i=4), z_planes[b][:].rearrange("p t (c i) -> p c t i", i=4))
+            woven.append(wv)
+        z_codes, z_scales = [], []
+        for b in range(2):
+            codes = keep.tile([P, HALF], U32, name=f"z_codes{b}", align_bytes=64)
+            plane = keep.tile([P, HALF], U8, name=f"z_plane{b}", align_bytes=64)
+            nc.vector.quantize_mx(codes[:].bitcast(FP8X4), plane[:], woven[b][:].rearrange("p c t -> p (c t)"))
+            z_codes.append(codes)
+            z_scales.append(plane)
+
+        out_rows = out.rearrange("(p t) w -> t p w", t=PACK)
+        halves = [slice(b * HALF, (b + 1) * HALF) for b in range(2)]
+        list_halves = [slice(16 * b, 16 * (b + 1)) for b in range(2)]
+
+        def scores(t):
+            cols = slice(t * P, (t + 1) * P)
+            s = keep.tile([P, S], F32, name=f"s{t}")
+            accs = [psum.tile([P, HALF], F32, name=f"s_acc{t}_{b}", tag=f"s_acc{(2 * t + b) % 4}") for b in range(2)]
+            for b in range(2):
+                nc.tensor.matmul_mx(accs[b][:], lhsT=xc_w[:, cols].bitcast(FP8X4), lhsT_scale=xc_plane[:, cols],
+                                    rhs=z_codes[b][:].bitcast(FP8X4), rhs_scale=z_scales[b][:], start=True, stop=True)
+                nc.scalar.activation(s[:, halves[b]], accs[b][:], ACT.Copy, scale=SIXTEENTH)
+            g = keep.tile([P, S], F32, name=f"g{t}")
+            for b in range(2):
+                nc.scalar.activation(g[:, halves[b]], s[:].indirect(n5_t[:, list_halves[b]]), ACT.Copy)
+            return s, g
+
+        def gap(t):
+            s, g = scores(t)
+            diff = keep.tile([P, S], F32, name=f"diff{t}")
+            nc.vector.tensor_tensor(diff[:], g[:], s[:], ALU.subtract)
+            return s, g, diff
+
+        def put(t, s, g, diff):
+            rise = keep.tile([P, S], F32, name=f"rise{t}")
+            fall = keep.tile([P, S], F32, name=f"fall{t}")
+            nc.scalar.activation(rise[:], diff[:], ACT.Relu)
+            nc.scalar.activation(fall[:], rise[:], ACT.Copy, scale=-1.0)
+            nc.vector.tensor_tensor(pages[t][:].indirect(n3_t[:]), s[:], rise[:], ALU.add)
+            nc.vector.tensor_tensor(pages[t][:].indirect(n4_t[:]), g[:], fall[:], ALU.add)
+            nc.sync.dma_start(out_rows[t], pages[t][:])
+
+        s, g = scores(0)
+        up = keep.tile([P, S], F32, name="up")
+        dn = keep.tile([P, S], F32, name="dn")
+        for b in range(2):
+            nc.vector.tensor_tensor(up[:, halves[b]], s[:, halves[b]], g[:, halves[b]], ALU.max)
+            nc.vector.tensor_copy(pages[0][:].indirect(n3_t[:, list_halves[b]]), up[:, halves[b]])
+        nc.vector.tensor_tensor(dn[:], s[:], g[:], ALU.min)
+        nc.vector.tensor_copy(pages[0][:].indirect(n4_t[:]), dn[:])
+        nc.sync.dma_start(out_rows[0], pages[0][:])
+
+        ahead = gap(1)
+        for t in range(1, PACK):
+            now = ahead
+            if t + 1 < PACK:
+                ahead = gap(t + 1)
+            put(t, *now)

@@ -1,6 +1,7 @@
 from contextlib import ExitStack
 
 import concourse.mybir as mybir
+from concourse.masks import make_identity
 
 K, T, S, G, H, W, C, U = 512, 1024, 512, 2048, 512, 256, 512, 1024
 FLOPS = 2 * K * H * S + 2 * K * C * S
@@ -42,17 +43,21 @@ def tile_picked_hpqcfillpagmx_none_p_kernel(tc, x_words, x_scales, d_words, d_sc
             nc.sync.dma_start(tile[:].bitcast(I32), src[0].rearrange("p n t -> p (n t)").bitcast(I32))
             return tile
 
-        d_sc = zeroed_bytes("d_sc", G, nc.gpsimd)
-        x_sc = zeroed_bytes("x_sc", T, nc.vector)
-        k1_t = load_list("k1_t", k1)
-        nc.sync.dma_start(d_sc[0:P:8, :].bitcast(I32), d_scales[0].bitcast(I32))
+        def load_scale_rows(name, src, width):
+            tile = keep.tile([P, width], U8, name=name, align_bytes=64)
+            rows = src[0].bitcast(I32)
+            nc.sync.dma_start(tile[:].bitcast(I32), rows.unsqueeze(1).to_broadcast([16, 8, width // 4]))
+            return tile
+
         offs_t = load_list("offs_t", offs)
-        nc.sync.dma_start(x_sc[0:P:8, :].bitcast(I32), x_scales[0].bitcast(I32))
+        x_sc = load_scale_rows("x_sc", x_scales, T)
+        k1_t = load_list("k1_t", k1)
+        d_sc = load_scale_rows("d_sc", d_scales, G)
+        cand_t = load_list("cand_t", cand)
         x_w = load_words("x_w", x_words, T)
         d_w = load_words("d_w", d_words, G)
         n1_t = load_list("n1_t", n1)
         n2_t = load_list("n2_t", n2)
-        cand_t = load_list("cand_t", cand)
         gs_t = keep.tile([P, PACK], F32, name="gs_t")
         nc.gpsimd.dma_start(gs_t[:], gs.rearrange("(p t) o -> p (t o)", t=PACK))
         n5_t = load_list("n5_t", n5)
@@ -65,9 +70,9 @@ def tile_picked_hpqcfillpagmx_none_p_kernel(tc, x_words, x_scales, d_words, d_sc
                 queues[r % len(queues)].dma_start(plane[r:P:32, :].bitcast(I32), src[8 * r : P : 32, :].bitcast(I32))
             return plane
 
-        picked_sc = keep.tile([P, H + S], U8, name="picked_sc", tag="picked_bytes", align_bytes=64)
-        nc.vector.tensor_copy(picked_sc[:, :H], d_sc[:].indirect(k1_t[:]))
+        picked_sc = keep.tile([P, H + S], U8, name="picked_sc", tag="after_moves", align_bytes=64)
         nc.vector.tensor_copy(picked_sc[:, H:], x_sc[:].indirect(offs_t[:]))
+        nc.vector.tensor_copy(picked_sc[:, :H], d_sc[:].indirect(k1_t[:]))
         placed_sc = place_rows("placed_sc", picked_sc, (nc.sync, nc.scalar))
         xq_w = keep.tile([P, S], U32, name="xq_w", align_bytes=64)
         nc.vector.tensor_copy(xq_w[:], x_w[:].indirect(offs_t[:]))
@@ -78,53 +83,58 @@ def tile_picked_hpqcfillpagmx_none_p_kernel(tc, x_words, x_scales, d_words, d_sc
         dk_plane = keep.tile([P, H], U8, name="dk_plane", align_bytes=64)
         nc.vector.tensor_copy(dk_plane[:].rearrange("p (t m) -> p t m", t=PACK), placed_sc[:, :H].rearrange("p (m t) -> p t m", t=PACK))
 
+        ident = keep.tile([P, P], F32, name="ident")
+        make_identity(nc, ident[:])
         pages = []
         for t in range(PACK):
             page = keep.tile([P, U], F32, name=f"page{t}")
             nc.gpsimd.memset(page[:], 0.0)
             pages.append(page)
 
-        h_acc = []
-        for t in range(PACK):
-            cols = slice(t * P, (t + 1) * P)
-            acc = psum.tile([P, S], F32, name=f"h_acc{t}")
-            nc.tensor.matmul_mx(acc[:], lhsT=dk_w_dealt[:, cols].bitcast(FP8X4), lhsT_scale=dk_plane[:, cols],
-                                rhs=xq_w[:].bitcast(FP8X4), rhs_scale=placed_sc[:, H:], start=True, stop=True)
-            h_acc.append(acc)
-
-        xc_sc = keep.tile([P, C], U8, name="xc_sc", tag="picked_bytes", align_bytes=64)
+        xc_sc = keep.tile([P, C], U8, name="xc_sc", align_bytes=64)
         nc.vector.tensor_copy(xc_sc[:].rearrange("p (t m) -> p m t", t=PACK), x_sc[:].indirect(cand_t[:]))
         xc_plane = place_rows("xc_plane", xc_sc, (nc.sync,))
 
+        xc_w = keep.tile([P, C], U32, name="xc_w", tag="after_moves", align_bytes=64)
+        nc.vector.tensor_copy(xc_w[:].rearrange("p (t m) -> p m t", t=PACK), x_w[:].indirect(cand_t[:]))
+
         hs = []
         for t in range(PACK):
+            cols = slice(t * P, (t + 1) * P)
+            acc = psum.tile([P, S], F32, name=f"h_acc{t}", tag=f"bank{1 if t == 1 else 0}")
+            nc.tensor.matmul_mx(acc[:], lhsT=dk_w_dealt[:, cols].bitcast(FP8X4), lhsT_scale=dk_plane[:, cols],
+                                rhs=xq_w[:].bitcast(FP8X4), rhs_scale=placed_sc[:, H:], start=True, stop=True)
             h = keep.tile([P, S], F32, name=f"h{t}")
-            if t in (1, 2):
-                nc.vector.tensor_scalar_mul(h[:], h_acc[t][:], SIXTEENTH)
+            if t == 1:
+                nc.vector.tensor_scalar_mul(h[:], acc[:], SIXTEENTH)
             else:
-                nc.scalar.activation(h[:], h_acc[t][:], ACT.Copy, scale=SIXTEENTH)
+                nc.scalar.activation(h[:], acc[:], ACT.Copy, scale=SIXTEENTH)
             hs.append(h)
             pa = keep.tile([P, W], F32, name=f"pa{t}")
             pb = keep.tile([P, W], F32, name=f"pb{t}")
             nc.scalar.activation(pa[:], h[:].indirect(n1_t[:]), ACT.Copy)
-            nc.scalar.activation(pb[:], h[:].indirect(n2_t[:]), ACT.Copy)
+            if t == 0:
+                nc.vector.tensor_copy(pb[:], h[:].indirect(n2_t[:]))
+            else:
+                nc.scalar.activation(pb[:], h[:].indirect(n2_t[:]), ACT.Copy)
             ra = keep.tile([P, W], F32, name=f"ra{t}", align_bytes=64)
             nc.vector.tensor_tensor(ra[:], pa[:], pb[:], ALU.max)
             nc.vector.tensor_copy(h[:].indirect(n1_t[:]), ra[:])
 
-        xc_w = keep.tile([P, C], U32, name="xc_w", tag=f"ra{PACK - 1}", align_bytes=64)
-        nc.vector.tensor_copy(xc_w[:].rearrange("p (t m) -> p m t", t=PACK), x_w[:].indirect(cand_t[:]))
-
-        z_planes = [keep.tile([P, PACK, HALF], BF16, name=f"z_planes{b}", align_bytes=64) for b in range(2)]
+        z_planes = keep.tile([P, PACK, S], BF16, name="z_planes", align_bytes=64)
         for t in range(PACK):
-            for b in range(2):
-                nc.scalar.activation(z_planes[b][:, t, :], hs[t][:, b * HALF : (b + 1) * HALF], ACT.Copy, scale=gs_t[:, t : t + 1])
+            pieces = 2 if t == PACK - 1 else 1
+            for b in range(pieces):
+                cols = slice(b * S // pieces, (b + 1) * S // pieces)
+                nc.scalar.activation(z_planes[:, t, cols], hs[t][:, cols], ACT.Copy, scale=gs_t[:, t : t + 1])
 
-        woven = []
-        for b in range(2):
-            wv = keep.tile([P, HALF, PACK], BF16, name=f"woven{b}", align_bytes=64)
-            nc.vector.tensor_copy(wv[:].rearrange("p (c i) t -> p c t i", i=4), z_planes[b][:].rearrange("p t (c i) -> p c t i", i=4))
-            woven.append(wv)
+        def weave(copy, dst, dst_cols, src_cols):
+            copy(dst[:, dst_cols, :].rearrange("p (c i) t -> p c t i", i=4), z_planes[:, :, src_cols].rearrange("p t (c i) -> p c t i", i=4))
+
+        woven = [keep.tile([P, HALF, PACK], BF16, name=f"woven{b}", align_bytes=64) for b in range(2)]
+        weave(nc.vector.tensor_copy, woven[0], slice(0, HALF), slice(0, HALF))
+        weave(nc.scalar.copy, woven[1], slice(HALF // 2, HALF), slice(S - HALF // 2, S))
+        weave(nc.vector.tensor_copy, woven[1], slice(0, HALF // 2), slice(HALF, HALF + HALF // 2))
         z_codes, z_scales = [], []
         for b in range(2):
             codes = keep.tile([P, HALF], U32, name=f"z_codes{b}", align_bytes=64)
@@ -137,47 +147,55 @@ def tile_picked_hpqcfillpagmx_none_p_kernel(tc, x_words, x_scales, d_words, d_sc
         halves = [slice(b * HALF, (b + 1) * HALF) for b in range(2)]
         list_halves = [slice(16 * b, 16 * (b + 1)) for b in range(2)]
 
-        def scores(t):
+        def scores(t, banks, pieces):
             cols = slice(t * P, (t + 1) * P)
             s = keep.tile([P, S], F32, name=f"s{t}")
-            accs = [psum.tile([P, HALF], F32, name=f"s_acc{t}_{b}", tag=f"s_acc{(2 * t + b) % 4}") for b in range(2)]
+            width = S // len(banks)
+            accs = [psum.tile([P, width], F32, name=f"s_acc{t}_{i}", tag=f"bank{bank}") for i, bank in enumerate(banks)]
             for b in range(2):
-                nc.tensor.matmul_mx(accs[b][:], lhsT=xc_w[:, cols].bitcast(FP8X4), lhsT_scale=xc_plane[:, cols],
+                acc = accs[b][:] if len(banks) == 2 else accs[0][:, halves[b]]
+                nc.tensor.matmul_mx(acc, lhsT=xc_w[:, cols].bitcast(FP8X4), lhsT_scale=xc_plane[:, cols],
                                     rhs=z_codes[b][:].bitcast(FP8X4), rhs_scale=z_scales[b][:], start=True, stop=True)
-                nc.scalar.activation(s[:, halves[b]], accs[b][:], ACT.Copy, scale=SIXTEENTH)
+            for i, acc in enumerate(accs):
+                nc.scalar.activation(s[:, i * width : (i + 1) * width], acc[:], ACT.Copy, scale=SIXTEENTH)
             g = keep.tile([P, S], F32, name=f"g{t}")
-            for b in range(2):
-                nc.scalar.activation(g[:, halves[b]], s[:].indirect(n5_t[:, list_halves[b]]), ACT.Copy)
-            return s, g
+            for lo, hi in pieces:
+                nc.scalar.activation(g[:, lo:hi], s[:].indirect(n5_t[:, lo // 16 : hi // 16]), ACT.Copy)
+            return s, g, accs
+
+        blocks = [slice(c * P, (c + 1) * P) for c in range(S // P)]
 
         def gap(t):
-            s, g = scores(t)
-            diff = keep.tile([P, S], F32, name=f"diff{t}")
-            nc.vector.tensor_tensor(diff[:], g[:], s[:], ALU.subtract)
-            return s, g, diff
-
-        def put(t, s, g, diff):
+            s, g, accs = scores(t, [6], [(0, HALF), (HALF, S)])
+            minus_s = keep.tile([P, S], F32, name=f"minus_s{t}")
+            nc.scalar.activation(minus_s[:], accs[0][:], ACT.Copy, scale=-SIXTEENTH)
+            diff_t = psum.tile([P, S], F32, name=f"diff_t{t}", tag=f"bank{2 + t % 2}")
+            terms = [(term, block) for term in (g, minus_s) for block in blocks]
+            for i, (term, block) in enumerate(terms):
+                nc.tensor.matmul(diff_t[:, block], lhsT=term[:, block], rhs=ident[:], is_transpose=True, start=(i == 0), stop=(i == len(terms) - 1))
+            rise_t = keep.tile([P, S], F32, name=f"rise_t{t}")
+            nc.scalar.activation(rise_t[:], diff_t[:], ACT.Relu)
+            back = psum.tile([P, S], F32, name=f"back{t}", tag=f"bank{4 + t % 2}")
+            for block in blocks:
+                nc.tensor.transpose(back[:, block], rise_t[:, block], ident[:])
             rise = keep.tile([P, S], F32, name=f"rise{t}")
             fall = keep.tile([P, S], F32, name=f"fall{t}")
-            nc.scalar.activation(rise[:], diff[:], ACT.Relu)
-            nc.scalar.activation(fall[:], rise[:], ACT.Copy, scale=-1.0)
+            nc.scalar.activation(rise[:], back[:], ACT.Copy)
+            nc.scalar.activation(fall[:], back[:], ACT.Copy, scale=-1.0)
             nc.vector.tensor_tensor(pages[t][:].indirect(n3_t[:]), s[:], rise[:], ALU.add)
             nc.vector.tensor_tensor(pages[t][:].indirect(n4_t[:]), g[:], fall[:], ALU.add)
             nc.sync.dma_start(out_rows[t], pages[t][:])
 
-        s, g = scores(0)
+        first_pieces = [(0, 128), (128, HALF), (HALF, S)]
+        s, g, accs0 = scores(0, [5, 6], first_pieces)
         up = keep.tile([P, S], F32, name="up")
         dn = keep.tile([P, S], F32, name="dn")
-        for b in range(2):
-            nc.vector.tensor_tensor(up[:, halves[b]], s[:, halves[b]], g[:, halves[b]], ALU.max)
-            nc.vector.tensor_copy(pages[0][:].indirect(n3_t[:, list_halves[b]]), up[:, halves[b]])
+        for lo, hi in first_pieces:
+            nc.vector.tensor_tensor(up[:, lo:hi], s[:, lo:hi], g[:, lo:hi], ALU.max)
+            nc.vector.tensor_copy(pages[0][:].indirect(n3_t[:, lo // 16 : hi // 16]), up[:, lo:hi])
         nc.vector.tensor_tensor(dn[:], s[:], g[:], ALU.min)
         nc.vector.tensor_copy(pages[0][:].indirect(n4_t[:]), dn[:])
         nc.sync.dma_start(out_rows[0], pages[0][:])
 
-        ahead = gap(1)
         for t in range(1, PACK):
-            now = ahead
-            if t + 1 < PACK:
-                ahead = gap(t + 1)
-            put(t, *now)
+            gap(t)

@@ -74,6 +74,10 @@ def tile_picked_hpqcfillpagmx_none_p_kernel(tc, x_words, x_scales, d_words, d_sc
         nc.vector.tensor_copy(picked_sc[:, H:], x_sc[:].indirect(offs_t[:]))
         nc.vector.tensor_copy(picked_sc[:, :H], d_sc[:].indirect(k1_t[:]))
         placed_sc = place_rows("placed_sc", picked_sc, (nc.sync, nc.scalar))
+        xc_sc = keep.tile([P, C], U8, name="xc_sc", align_bytes=64)
+        nc.vector.tensor_copy(xc_sc[:].rearrange("p (t a u) -> p a t u", t=PACK, u=8), x_sc[:].indirect(cand_t[:]))
+        xc_plane = place_rows("xc_plane", xc_sc, (nc.sync,))
+
         xq_w = keep.tile([P, S], U32, name="xq_w", align_bytes=64)
         nc.vector.tensor_copy(xq_w[:], x_w[:].indirect(offs_t[:]))
         dk_w = keep.tile([P, H], U32, name="dk_w", align_bytes=64)
@@ -91,86 +95,92 @@ def tile_picked_hpqcfillpagmx_none_p_kernel(tc, x_words, x_scales, d_words, d_sc
             nc.gpsimd.memset(page[:], 0.0)
             pages.append(page)
 
-        xc_sc = keep.tile([P, C], U8, name="xc_sc", align_bytes=64)
-        nc.vector.tensor_copy(xc_sc[:].rearrange("p (t m) -> p m t", t=PACK), x_sc[:].indirect(cand_t[:]))
-        xc_plane = place_rows("xc_plane", xc_sc, (nc.sync,))
-
         xc_w = keep.tile([P, C], U32, name="xc_w", tag="after_moves", align_bytes=64)
-        nc.vector.tensor_copy(xc_w[:].rearrange("p (t m) -> p m t", t=PACK), x_w[:].indirect(cand_t[:]))
+        nc.vector.tensor_copy(xc_w[:].rearrange("p (t a u) -> p a t u", t=PACK, u=8), x_w[:].indirect(cand_t[:]))
 
         hs = []
         for t in range(PACK):
             cols = slice(t * P, (t + 1) * P)
-            acc = psum.tile([P, S], F32, name=f"h_acc{t}", tag=f"bank{1 if t == 1 else 0}")
-            nc.tensor.matmul_mx(acc[:], lhsT=dk_w_dealt[:, cols].bitcast(FP8X4), lhsT_scale=dk_plane[:, cols],
-                                rhs=xq_w[:].bitcast(FP8X4), rhs_scale=placed_sc[:, H:], start=True, stop=True)
             h = keep.tile([P, S], F32, name=f"h{t}")
-            if t == 1:
-                nc.vector.tensor_scalar_mul(h[:], acc[:], SIXTEENTH)
+
+            def product(lo, hi, bank):
+                acc = psum.tile([P, hi - lo], F32, name=f"h_acc{t}_{lo}", tag=f"bank{bank}")
+                nc.tensor.matmul_mx(acc[:], lhsT=dk_w_dealt[:, cols].bitcast(FP8X4), lhsT_scale=dk_plane[:, cols],
+                                    rhs=xq_w[:, lo:hi].bitcast(FP8X4), rhs_scale=placed_sc[:, H + lo : H + hi], start=True, stop=True)
+                return acc
+
+            if t == 0:
+                left, right = product(0, HALF, 0), product(HALF, S, 1)
+                h_twin = keep.tile([P, S], F32, name="h_twin")
+                nc.scalar.activation(h[:, :HALF], left[:], ACT.Copy, scale=SIXTEENTH)
+                nc.vector.tensor_scalar_mul(h_twin[:, HALF:], right[:], SIXTEENTH)
+                nc.scalar.activation(h[:, HALF:], right[:], ACT.Copy, scale=SIXTEENTH)
+                nc.vector.tensor_scalar_mul(h_twin[:, :HALF], left[:], SIXTEENTH)
             else:
-                nc.scalar.activation(h[:], acc[:], ACT.Copy, scale=SIXTEENTH)
+                nc.scalar.activation(h[:], product(0, S, 0)[:], ACT.Copy, scale=SIXTEENTH)
             hs.append(h)
             pa = keep.tile([P, W], F32, name=f"pa{t}")
-            pb = keep.tile([P, W], F32, name=f"pb{t}")
+            pb = keep.tile([P, W], F32, name=f"pb{t}", align_bytes=64)
             nc.scalar.activation(pa[:], h[:].indirect(n1_t[:]), ACT.Copy)
             if t == 0:
-                nc.vector.tensor_copy(pb[:], h[:].indirect(n2_t[:]))
+                nc.vector.tensor_copy(pb[:], h_twin[:].indirect(n2_t[:]))
             else:
                 nc.scalar.activation(pb[:], h[:].indirect(n2_t[:]), ACT.Copy)
             ra = keep.tile([P, W], F32, name=f"ra{t}", align_bytes=64)
             nc.vector.tensor_tensor(ra[:], pa[:], pb[:], ALU.max)
             nc.vector.tensor_copy(h[:].indirect(n1_t[:]), ra[:])
 
-        z_planes = keep.tile([P, PACK, S], BF16, name="z_planes", align_bytes=64)
+        z_planes = keep.tile([P, PACK, S], BF16, name="z_planes", tag=f"pb{PACK - 1}", align_bytes=64)
         for t in range(PACK):
             pieces = 2 if t == PACK - 1 else 1
             for b in range(pieces):
                 cols = slice(b * S // pieces, (b + 1) * S // pieces)
                 nc.scalar.activation(z_planes[:, t, cols], hs[t][:, cols], ACT.Copy, scale=gs_t[:, t : t + 1])
 
-        def weave(copy, dst, dst_cols, src_cols):
-            copy(dst[:, dst_cols, :].rearrange("p (c i) t -> p c t i", i=4), z_planes[:, :, src_cols].rearrange("p t (c i) -> p c t i", i=4))
+        chunks = [(0, 256, nc.vector.tensor_copy), (256, 384, nc.vector.tensor_copy), (384, 512, nc.scalar.copy)]
+        woven = []
+        for lo, hi, copy in chunks:
+            wv = keep.tile([P, hi - lo, PACK], BF16, name=f"woven{lo}", align_bytes=64)
+            copy(wv[:].rearrange("p (c i) t -> p c t i", i=4), z_planes[:, :, lo:hi].rearrange("p t (c i) -> p c t i", i=4))
+            woven.append(wv)
+        z_mx = []
+        for (lo, hi, copy), wv in zip(chunks, woven):
+            codes = keep.tile([P, hi - lo], U32, name=f"z_codes{lo}", align_bytes=64)
+            plane = keep.tile([P, hi - lo], U8, name=f"z_plane{lo}", align_bytes=64)
+            nc.vector.quantize_mx(codes[:].bitcast(FP8X4), plane[:], wv[:].rearrange("p c t -> p (c t)"))
+            z_mx.append((lo, hi, codes, plane))
 
-        woven = [keep.tile([P, HALF, PACK], BF16, name=f"woven{b}", align_bytes=64) for b in range(2)]
-        weave(nc.vector.tensor_copy, woven[0], slice(0, HALF), slice(0, HALF))
-        weave(nc.scalar.copy, woven[1], slice(HALF // 2, HALF), slice(S - HALF // 2, S))
-        weave(nc.vector.tensor_copy, woven[1], slice(0, HALF // 2), slice(HALF, HALF + HALF // 2))
-        z_codes, z_scales = [], []
-        for b in range(2):
-            codes = keep.tile([P, HALF], U32, name=f"z_codes{b}", align_bytes=64)
-            plane = keep.tile([P, HALF], U8, name=f"z_plane{b}", align_bytes=64)
-            nc.vector.quantize_mx(codes[:].bitcast(FP8X4), plane[:], woven[b][:].rearrange("p c t -> p (c t)"))
-            z_codes.append(codes)
-            z_scales.append(plane)
-
-        out_rows = out.rearrange("(p t) w -> t p w", t=PACK)
+        out_rows = out.rearrange("(a t u) w -> t a u w", t=PACK, u=8)
         halves = [slice(b * HALF, (b + 1) * HALF) for b in range(2)]
         list_halves = [slice(16 * b, 16 * (b + 1)) for b in range(2)]
 
         def scores(t, banks, pieces):
             cols = slice(t * P, (t + 1) * P)
             s = keep.tile([P, S], F32, name=f"s{t}")
-            width = S // len(banks)
-            accs = [psum.tile([P, width], F32, name=f"s_acc{t}_{i}", tag=f"bank{bank}") for i, bank in enumerate(banks)]
-            for b in range(2):
-                acc = accs[b][:] if len(banks) == 2 else accs[0][:, halves[b]]
-                nc.tensor.matmul_mx(acc, lhsT=xc_w[:, cols].bitcast(FP8X4), lhsT_scale=xc_plane[:, cols],
-                                    rhs=z_codes[b][:].bitcast(FP8X4), rhs_scale=z_scales[b][:], start=True, stop=True)
-            for i, acc in enumerate(accs):
-                nc.scalar.activation(s[:, i * width : (i + 1) * width], acc[:], ACT.Copy, scale=SIXTEENTH)
+            accs = {bank: psum.tile([P, S], F32, name=f"s_acc{t}_{bank}", tag=f"bank{bank}") for bank in set(banks)}
+            for bank, (lo, hi, codes, plane) in zip(banks, z_mx):
+                nc.tensor.matmul_mx(accs[bank][:, lo:hi], lhsT=xc_w[:, cols].bitcast(FP8X4), lhsT_scale=xc_plane[:, cols],
+                                    rhs=codes[:].bitcast(FP8X4), rhs_scale=plane[:], start=True, stop=True)
+            if t == 0:
+                for bank, (lo, hi, codes, plane) in zip(banks, z_mx):
+                    nc.scalar.activation(s[:, lo:hi], accs[bank][:, lo:hi], ACT.Copy, scale=SIXTEENTH)
+            else:
+                nc.scalar.activation(s[:], accs[banks[0]][:], ACT.Copy, scale=SIXTEENTH)
+            minus_s = None
+            if t > 0:
+                minus_s = keep.tile([P, S], F32, name=f"minus_s{t}")
+                nc.scalar.activation(minus_s[:], accs[banks[0]][:], ACT.Copy, scale=-SIXTEENTH)
             g = keep.tile([P, S], F32, name=f"g{t}")
             for lo, hi in pieces:
                 nc.scalar.activation(g[:, lo:hi], s[:].indirect(n5_t[:, lo // 16 : hi // 16]), ACT.Copy)
-            return s, g, accs
+            return s, g, minus_s
 
         blocks = [slice(c * P, (c + 1) * P) for c in range(S // P)]
 
         def gap(t):
-            s, g, accs = scores(t, [6], [(0, HALF), (HALF, S)])
-            minus_s = keep.tile([P, S], F32, name=f"minus_s{t}")
-            nc.scalar.activation(minus_s[:], accs[0][:], ACT.Copy, scale=-SIXTEENTH)
+            s, g, minus_s = scores(t, [6, 6, 6], [(0, HALF), (HALF, S)])
             diff_t = psum.tile([P, S], F32, name=f"diff_t{t}", tag=f"bank{2 + t % 2}")
-            terms = [(term, block) for term in (g, minus_s) for block in blocks]
+            terms = [(term, block) for term in (minus_s, g) for block in blocks]
             for i, (term, block) in enumerate(terms):
                 nc.tensor.matmul(diff_t[:, block], lhsT=term[:, block], rhs=ident[:], is_transpose=True, start=(i == 0), stop=(i == len(terms) - 1))
             rise_t = keep.tile([P, S], F32, name=f"rise_t{t}")
@@ -187,7 +197,7 @@ def tile_picked_hpqcfillpagmx_none_p_kernel(tc, x_words, x_scales, d_words, d_sc
             nc.sync.dma_start(out_rows[t], pages[t][:])
 
         first_pieces = [(0, 128), (128, HALF), (HALF, S)]
-        s, g, accs0 = scores(0, [5, 6], first_pieces)
+        s, g, accs0 = scores(0, [5, 7, 6], first_pieces)
         up = keep.tile([P, S], F32, name="up")
         dn = keep.tile([P, S], F32, name="dn")
         for lo, hi in first_pieces:

@@ -54,10 +54,10 @@ def tile_picked_hpqcfillpagmx_none_p_kernel(tc, x_words, x_scales, d_words, d_sc
         k1_t = load_list("k1_t", k1)
         d_sc = load_scale_rows("d_sc", d_scales, G)
         cand_t = load_list("cand_t", cand)
-        x_w = load_words("x_w", x_words, T)
-        d_w = load_words("d_w", d_words, G)
         n1_t = load_list("n1_t", n1)
         n2_t = load_list("n2_t", n2)
+        d_w = load_words("d_w", d_words, G)
+        x_w = load_words("x_w", x_words, T)
         gs_t = keep.tile([P, PACK], F32, name="gs_t")
         nc.gpsimd.dma_start(gs_t[:], gs.rearrange("(p t) o -> p (t o)", t=PACK))
         n5_t = load_list("n5_t", n5)
@@ -78,12 +78,12 @@ def tile_picked_hpqcfillpagmx_none_p_kernel(tc, x_words, x_scales, d_words, d_sc
         nc.vector.tensor_copy(xc_sc[:].rearrange("p (t a u) -> p a t u", t=PACK, u=8), x_sc[:].indirect(cand_t[:]))
         xc_plane = place_rows("xc_plane", xc_sc, (nc.sync,))
 
-        xq_w = keep.tile([P, S], U32, name="xq_w", align_bytes=64)
-        nc.vector.tensor_copy(xq_w[:], x_w[:].indirect(offs_t[:]))
         dk_w = keep.tile([P, H], U32, name="dk_w", align_bytes=64)
         nc.vector.tensor_copy(dk_w[:], d_w[:].indirect(k1_t[:]))
         dk_w_dealt = keep.tile([P, H], U32, name="dk_w_dealt", align_bytes=64)
         nc.vector.tensor_copy(dk_w_dealt[:].rearrange("p (t m) -> p t m", t=PACK).bitcast(I32), dk_w[:].bitcast(I32).rearrange("p (m t) -> p t m", t=PACK))
+        xq_w = keep.tile([P, S], U32, name="xq_w", align_bytes=64)
+        nc.vector.tensor_copy(xq_w[:], x_w[:].indirect(offs_t[:]))
         dk_plane = keep.tile([P, H], U8, name="dk_plane", align_bytes=64)
         nc.vector.tensor_copy(dk_plane[:].rearrange("p (t m) -> p t m", t=PACK), placed_sc[:, :H].rearrange("p (m t) -> p t m", t=PACK))
 

from contextlib import ExitStack

import concourse.mybir as mybir
from concourse.masks import make_identity

K, T, S, G, H, W, C, U = 512, 1024, 512, 2048, 512, 256, 512, 1024
FLOPS = 2 * K * H * S + 2 * K * C * S

F32 = mybir.dt.float32
BF16 = mybir.dt.bfloat16
I32 = mybir.dt.int32
U32 = mybir.dt.uint32
U16 = mybir.dt.uint16
U8 = mybir.dt.uint8
FP8X4 = mybir.dt.float8_e4m3fn_x4
ACT = mybir.ActivationFunctionType
ALU = mybir.AluOpType

P = 128
PACK = 4
HALF = S // 2
SIXTEENTH = 0.0625


def tile_picked_hpqcfillpagmx_none_p_kernel(tc, x_words, x_scales, d_words, d_scales, gs, offs, k1, n1, n2, cand, n3, n4, n5, out):
    nc = tc.nc
    with ExitStack() as ctx:
        keep = ctx.enter_context(tc.tile_pool(name="keep", bufs=1))
        psum = ctx.enter_context(tc.psum_pool(name="psum", bufs=1))

        def load_list(name, src):
            tile = keep.tile([P, src.shape[1]], U16, name=name)
            nc.sync.dma_start(tile[:], src)
            return tile

        def zeroed_bytes(name, width, engine):
            tile = keep.tile([P, width], U8, name=name, align_bytes=64)
            engine.memset(tile[:].bitcast(I32), 0)
            return tile

        def load_words(name, src, width):
            tile = keep.tile([P, width], U32, name=name, align_bytes=64)
            nc.sync.dma_start(tile[:].bitcast(I32), src[0].rearrange("p n t -> p (n t)").bitcast(I32))
            return tile

        def load_scale_rows(name, src, width):
            tile = keep.tile([P, width], U8, name=name, align_bytes=64)
            rows = src[0].bitcast(I32)
            nc.sync.dma_start(tile[:].bitcast(I32), rows.unsqueeze(1).to_broadcast([16, 8, width // 4]))
            return tile

        offs_t = load_list("offs_t", offs)
        x_sc = load_scale_rows("x_sc", x_scales, T)
        k1_t = load_list("k1_t", k1)
        d_sc = load_scale_rows("d_sc", d_scales, G)
        cand_t = load_list("cand_t", cand)
        n1_t = load_list("n1_t", n1)
        n2_t = load_list("n2_t", n2)
        d_w = load_words("d_w", d_words, G)
        x_w = load_words("x_w", x_words, T)
        gs_t = keep.tile([P, PACK], F32, name="gs_t")
        nc.gpsimd.dma_start(gs_t[:], gs.rearrange("(p t) o -> p (t o)", t=PACK))
        n5_t = load_list("n5_t", n5)
        n3_t = load_list("n3_t", n3)
        n4_t = load_list("n4_t", n4)

        def place_rows(name, src, queues):
            plane = zeroed_bytes(name, src.shape[1], nc.vector)
            for r in range(4):
                queues[r % len(queues)].dma_start(plane[r:P:32, :].bitcast(I32), src[8 * r : P : 32, :].bitcast(I32))
            return plane

        picked_sc = keep.tile([P, H + S], U8, name="picked_sc", tag="after_moves", align_bytes=64)
        nc.vector.tensor_copy(picked_sc[:, H:], x_sc[:].indirect(offs_t[:]))
        nc.vector.tensor_copy(picked_sc[:, :H], d_sc[:].indirect(k1_t[:]))
        placed_sc = place_rows("placed_sc", picked_sc, (nc.sync, nc.scalar))
        xc_sc = keep.tile([P, C], U8, name="xc_sc", align_bytes=64)
        nc.vector.tensor_copy(xc_sc[:].rearrange("p (t a u) -> p a t u", t=PACK, u=8), x_sc[:].indirect(cand_t[:]))
        xc_plane = place_rows("xc_plane", xc_sc, (nc.sync,))

        dk_w = keep.tile([P, H], U32, name="dk_w", align_bytes=64)
        nc.vector.tensor_copy(dk_w[:], d_w[:].indirect(k1_t[:]))
        dk_w_dealt = keep.tile([P, H], U32, name="dk_w_dealt", align_bytes=64)
        nc.vector.tensor_copy(dk_w_dealt[:].rearrange("p (t m) -> p t m", t=PACK).bitcast(I32), dk_w[:].bitcast(I32).rearrange("p (m t) -> p t m", t=PACK))
        xq_w = keep.tile([P, S], U32, name="xq_w", align_bytes=64)
        nc.vector.tensor_copy(xq_w[:], x_w[:].indirect(offs_t[:]))
        dk_plane = keep.tile([P, H], U8, name="dk_plane", align_bytes=64)
        nc.vector.tensor_copy(dk_plane[:].rearrange("p (t m) -> p t m", t=PACK), placed_sc[:, :H].rearrange("p (m t) -> p t m", t=PACK))

        ident = keep.tile([P, P], F32, name="ident")
        make_identity(nc, ident[:])
        pages = []
        for t in range(PACK):
            page = keep.tile([P, U], F32, name=f"page{t}")
            nc.gpsimd.memset(page[:], 0.0)
            pages.append(page)

        xc_w = keep.tile([P, C], U32, name="xc_w", tag="after_moves", align_bytes=64)
        nc.vector.tensor_copy(xc_w[:].rearrange("p (t a u) -> p a t u", t=PACK, u=8), x_w[:].indirect(cand_t[:]))

        hs = []
        for t in range(PACK):
            cols = slice(t * P, (t + 1) * P)
            h = keep.tile([P, S], F32, name=f"h{t}")

            def product(lo, hi, bank):
                acc = psum.tile([P, hi - lo], F32, name=f"h_acc{t}_{lo}", tag=f"bank{bank}")
                nc.tensor.matmul_mx(acc[:], lhsT=dk_w_dealt[:, cols].bitcast(FP8X4), lhsT_scale=dk_plane[:, cols],
                                    rhs=xq_w[:, lo:hi].bitcast(FP8X4), rhs_scale=placed_sc[:, H + lo : H + hi], start=True, stop=True)
                return acc

            if t == 0:
                left, right = product(0, HALF, 0), product(HALF, S, 1)
                h_twin = keep.tile([P, S], F32, name="h_twin")
                nc.scalar.activation(h[:, :HALF], left[:], ACT.Copy, scale=SIXTEENTH)
                nc.vector.tensor_scalar_mul(h_twin[:, HALF:], right[:], SIXTEENTH)
                nc.scalar.activation(h[:, HALF:], right[:], ACT.Copy, scale=SIXTEENTH)
                nc.vector.tensor_scalar_mul(h_twin[:, :HALF], left[:], SIXTEENTH)
            else:
                nc.scalar.activation(h[:], product(0, S, 0)[:], ACT.Copy, scale=SIXTEENTH)
            hs.append(h)
            pa = keep.tile([P, W], F32, name=f"pa{t}")
            pb = keep.tile([P, W], F32, name=f"pb{t}", align_bytes=64)
            nc.scalar.activation(pa[:], h[:].indirect(n1_t[:]), ACT.Copy)
            if t == 0:
                nc.vector.tensor_copy(pb[:], h_twin[:].indirect(n2_t[:]))
            else:
                nc.scalar.activation(pb[:], h[:].indirect(n2_t[:]), ACT.Copy)
            ra = keep.tile([P, W], F32, name=f"ra{t}", align_bytes=64)
            nc.vector.tensor_tensor(ra[:], pa[:], pb[:], ALU.max)
            nc.vector.tensor_copy(h[:].indirect(n1_t[:]), ra[:])

        z_planes = keep.tile([P, PACK, S], BF16, name="z_planes", tag=f"pb{PACK - 1}", align_bytes=64)
        for t in range(PACK):
            pieces = 2 if t == PACK - 1 else 1
            for b in range(pieces):
                cols = slice(b * S // pieces, (b + 1) * S // pieces)
                nc.scalar.activation(z_planes[:, t, cols], hs[t][:, cols], ACT.Copy, scale=gs_t[:, t : t + 1])

        chunks = [(0, 256, nc.vector.tensor_copy), (256, 384, nc.vector.tensor_copy), (384, 512, nc.scalar.copy)]
        woven = []
        for lo, hi, copy in chunks:
            wv = keep.tile([P, hi - lo, PACK], BF16, name=f"woven{lo}", align_bytes=64)
            copy(wv[:].rearrange("p (c i) t -> p c t i", i=4), z_planes[:, :, lo:hi].rearrange("p t (c i) -> p c t i", i=4))
            woven.append(wv)
        z_mx = []
        for (lo, hi, copy), wv in zip(chunks, woven):
            codes = keep.tile([P, hi - lo], U32, name=f"z_codes{lo}", align_bytes=64)
            plane = keep.tile([P, hi - lo], U8, name=f"z_plane{lo}", align_bytes=64)
            nc.vector.quantize_mx(codes[:].bitcast(FP8X4), plane[:], wv[:].rearrange("p c t -> p (c t)"))
            z_mx.append((lo, hi, codes, plane))

        out_rows = out.rearrange("(a t u) w -> t a u w", t=PACK, u=8)
        halves = [slice(b * HALF, (b + 1) * HALF) for b in range(2)]
        list_halves = [slice(16 * b, 16 * (b + 1)) for b in range(2)]

        def scores(t, banks, pieces):
            cols = slice(t * P, (t + 1) * P)
            s = keep.tile([P, S], F32, name=f"s{t}")
            accs = {bank: psum.tile([P, S], F32, name=f"s_acc{t}_{bank}", tag=f"bank{bank}") for bank in set(banks)}
            for bank, (lo, hi, codes, plane) in zip(banks, z_mx):
                nc.tensor.matmul_mx(accs[bank][:, lo:hi], lhsT=xc_w[:, cols].bitcast(FP8X4), lhsT_scale=xc_plane[:, cols],
                                    rhs=codes[:].bitcast(FP8X4), rhs_scale=plane[:], start=True, stop=True)
            if t == 0:
                for bank, (lo, hi, codes, plane) in zip(banks, z_mx):
                    nc.scalar.activation(s[:, lo:hi], accs[bank][:, lo:hi], ACT.Copy, scale=SIXTEENTH)
            else:
                nc.scalar.activation(s[:], accs[banks[0]][:], ACT.Copy, scale=SIXTEENTH)
            minus_s = None
            if t > 0:
                minus_s = keep.tile([P, S], F32, name=f"minus_s{t}")
                nc.scalar.activation(minus_s[:], accs[banks[0]][:], ACT.Copy, scale=-SIXTEENTH)
            g = keep.tile([P, S], F32, name=f"g{t}")
            for lo, hi in pieces:
                nc.scalar.activation(g[:, lo:hi], s[:].indirect(n5_t[:, lo // 16 : hi // 16]), ACT.Copy)
            return s, g, minus_s

        blocks = [slice(c * P, (c + 1) * P) for c in range(S // P)]

        def gap(t):
            s, g, minus_s = scores(t, [6, 6, 6], [(0, HALF), (HALF, S)])
            diff_t = psum.tile([P, S], F32, name=f"diff_t{t}", tag=f"bank{2 + t % 2}")
            terms = [(term, block) for term in (minus_s, g) for block in blocks]
            for i, (term, block) in enumerate(terms):
                nc.tensor.matmul(diff_t[:, block], lhsT=term[:, block], rhs=ident[:], is_transpose=True, start=(i == 0), stop=(i == len(terms) - 1))
            rise_t = keep.tile([P, S], F32, name=f"rise_t{t}")
            nc.scalar.activation(rise_t[:], diff_t[:], ACT.Relu)
            back = psum.tile([P, S], F32, name=f"back{t}", tag=f"bank{4 + t % 2}")
            for block in blocks:
                nc.tensor.transpose(back[:, block], rise_t[:, block], ident[:])
            rise = keep.tile([P, S], F32, name=f"rise{t}")
            fall = keep.tile([P, S], F32, name=f"fall{t}")
            nc.scalar.activation(rise[:], back[:], ACT.Copy)
            nc.scalar.activation(fall[:], back[:], ACT.Copy, scale=-1.0)
            nc.vector.tensor_tensor(pages[t][:].indirect(n3_t[:]), s[:], rise[:], ALU.add)
            nc.vector.tensor_tensor(pages[t][:].indirect(n4_t[:]), g[:], fall[:], ALU.add)
            nc.sync.dma_start(out_rows[t], pages[t][:])

        first_pieces = [(0, 128), (128, HALF), (HALF, S)]
        s, g, accs0 = scores(0, [5, 7, 6], first_pieces)
        up = keep.tile([P, S], F32, name="up")
        dn = keep.tile([P, S], F32, name="dn")
        for lo, hi in first_pieces:
            nc.vector.tensor_tensor(up[:, lo:hi], s[:, lo:hi], g[:, lo:hi], ALU.max)
            nc.vector.tensor_copy(pages[0][:].indirect(n3_t[:, lo // 16 : hi // 16]), up[:, lo:hi])
        nc.vector.tensor_tensor(dn[:], s[:], g[:], ALU.min)
        nc.vector.tensor_copy(pages[0][:].indirect(n4_t[:]), dn[:])
        nc.sync.dma_start(out_rows[0], pages[0][:])

        for t in range(1, PACK):
            gap(t)
